import numpy as np
import ml_dtypes


def mxq(x, axis, fmt="e4m3"):
    dtype, down = {"e4m3": (ml_dtypes.float8_e4m3fn, 7), "e5m2": (ml_dtypes.float8_e5m2, 14)}[fmt]
    v = np.moveaxis(np.asarray(x, np.float32).astype(ml_dtypes.bfloat16).astype(np.float64), axis, -1)
    blocks = v.reshape(v.shape[:-1] + (-1, 32))
    amax = np.abs(blocks).max(-1, keepdims=True)
    byte = np.maximum(np.where(amax > 0, np.frexp(amax)[1] - 1 + 127, 0) - down, 1)
    scale = np.exp2(byte - 127.0)
    codes = (blocks / scale).astype(np.float32).astype(dtype).astype(np.float64)
    return np.moveaxis((codes * scale).reshape(v.shape), -1, axis)


WIDE = False


def mx_kscale(k):
    if not WIDE:
        return np.ones(k)
    levels = np.array([10, -10, 5, -5, 0])
    if k % 512:
        return np.exp2(np.random.permutation(np.resize(levels, k // 32))).repeat(32)
    a = np.empty((k // 512, 16))
    for p in range(k // 512):
        a[p, :8] = np.random.permutation(np.resize(levels, 8))
        for g in range(8):
            far = levels[np.abs(levels - a[p, g]) >= 10]
            a[p, g + 8] = far[np.random.randint(len(far))]
    return np.exp2(a.ravel()).repeat(32)


def f64(x):
    return np.asarray(x).astype(np.float64)


def striped(idx):
    return np.tile(np.asarray(idx).reshape(-1, 16).T, (8, 1)).astype(np.uint16)


def unstriped(offs):
    return offs[:16].T.reshape(-1).astype(np.int64)


E2M1 = np.array([0.0, 0.5, 1.0, 1.5, 2.0, 3.0, 4.0, 6.0, -0.0, -0.5, -1.0, -1.5, -2.0, -3.0, -4.0, -6.0])


def pack_weight(w, fmt):
    k, n = w.shape
    w = f64(np.asarray(w, np.float32).astype(ml_dtypes.bfloat16)).reshape(k // 32, 32, n)
    amax = np.abs(w).max(1)
    if fmt == "e4m3":
        byte = np.frexp(amax)[1] - 1 + 127 - 7
    else:
        mant, ex = np.frexp(amax / 6.0)
        byte = np.where(mant > 0.5, ex, ex - 1) + 127
    byte = np.clip(np.where(amax > 0, byte, 1), 1, 254)
    scaled = (w * np.exp2(127.0 - byte)[:, None, :]).reshape(k, n).astype(np.float32)
    by_word = np.ascontiguousarray(scaled.reshape(k // 512, 128, 4, n).transpose(0, 1, 3, 2))
    if fmt == "e4m3":
        words = by_word.astype(ml_dtypes.float8_e4m3fn).view(np.uint8)
    else:
        c = by_word.astype(ml_dtypes.float4_e2m1fn).view(np.uint8) & 0xF
        words = (c[..., 0::2] | (c[..., 1::2] << 4)).reshape(k // 512, 128, 2 * n)
    return np.ascontiguousarray(words), np.ascontiguousarray(byte.astype(np.uint8).reshape(k // 512, 16, n))


def unpack_weight(words, scales, fmt):
    g, _, n = scales.shape
    words = np.ascontiguousarray(words).reshape(g, 128, n, -1)
    if fmt == "e4m3":
        vals = words.view(ml_dtypes.float8_e4m3fn).astype(np.float64)
    else:
        nib = np.empty((g, 128, n, 4), np.uint8)
        nib[..., 0::2] = words & 0xF
        nib[..., 1::2] = words >> 4
        vals = E2M1[nib]
    vals = vals * np.repeat(np.exp2(scales.astype(np.float64) - 127.0), 8, axis=1)[..., None]
    return vals.transpose(0, 1, 3, 2).reshape(g * 512, n)


D, E, T, I, Q, G = 512, 512, 2048, 512, 128, 64


def setup_inputs():
    n = np.random.standard_normal
    idx = np.random.permutation(T)[:I]
    fd = mx_kscale(D)
    fe = mx_kscale(E)
    keysp = pack_weight(n((D, T)) / fd[:, None], "e2m1")
    valsp = pack_weight(n((E, T)) / fe[:, None], "e2m1")
    return {
        "query": (n((D, Q)) * 0.8 / np.sqrt(D) * fd[:, None]).astype(np.float32),
        "query2": (n((D, Q)) * 0.8 / np.sqrt(D) * fd[:, None]).astype(np.float32),
        "keys_words": keysp[0],
        "keys_scales": keysp[1],
        "gout": (n((E, Q)) * 1 / np.sqrt(E) * fe[:, None]).astype(np.float32),
        "vals_words": valsp[0],
        "vals_scales": valsp[1],
        "dquery": (n((D, Q)) * 1.0 / np.sqrt(D) * fd[:, None]).astype(np.float32),
        "base": (0.5 * n((Q, T))).astype(np.float32),
        "offs": striped(idx),
    }


def reference(query, query2, keys_words, keys_scales, gout, vals_words, vals_scales, dquery, base, offs):
    idx = unstriped(offs)
    keysu = unpack_weight(keys_words, keys_scales, "e2m1")
    valsu = unpack_weight(vals_words, vals_scales, "e2m1")
    queryq = mxq(f64(query), 0, "e4m3")
    keysidxg = keysu[:, idx]
    a = queryq.T @ keysidxg
    dqueryq = mxq(f64(dquery), 0, "e4m3")
    ta = dqueryq.T @ keysidxg
    query2q = mxq(f64(query2), 0, "e4m3")
    b = query2q.T @ keysidxg
    pa = np.exp(a)
    sa = pa.reshape(Q, G, I // G).sum(axis=2)
    z = np.sum(sa, axis=1, keepdims=True)
    pb = np.exp(b)
    sb = pb.reshape(Q, G, I // G).sum(axis=2)
    goutq = mxq(f64(gout), 0, "e4m3")
    valsidxg = valsu[:, idx]
    c0 = goutq.T @ valsidxg
    drr = c0 * pb
    dr = drr.reshape(Q, G, I // G).sum(axis=2)
    dz = np.sum(dr / sb * sa / np.square(z) * (-1.0), axis=1, keepdims=True)
    dsa = dr / sb / z + dz
    r1 = np.repeat(dsa, I // G, axis=1)
    tpa = ta * pa
    tsa = tpa.reshape(Q, G, I // G).sum(axis=2)
    tz = np.sum(tsa, axis=1, keepdims=True)
    tdz = np.sum((tsa * dr / sb - tz * z * 2.0 * dr / sb * sa / np.square(z)) / np.square(z) * (-1.0), axis=1, keepdims=True)
    tdsa = tz * dr / sb / np.square(z) * (-1.0) + tdz
    tr1 = np.repeat(tdsa, I // G, axis=1)
    tda = tr1 * pa + tpa * r1
    gs = tda * 512.0
    gf = np.zeros((Q, T))
    gf[:, idx] = gs
    y = f64(base) + gf
    return y

@@ -1,0 +1,201 @@
+import math
+from contextlib import ExitStack
+
+import concourse.mybir as mybir
+
+F32 = mybir.dt.float32
+BF16 = mybir.dt.bfloat16
+I32 = mybir.dt.int32
+U32 = mybir.dt.uint32
+U16 = mybir.dt.uint16
+U8 = mybir.dt.uint8
+FP8X4 = mybir.dt.float8_e4m3fn_x4
+FP4X4 = mybir.dt.float4_e2m1fn_x4
+ALU = mybir.AluOpType
+ACT = mybir.ActivationFunctionType
+AX = mybir.AxisListType
+
+P = 128
+PACK = 4
+POOL = 2048
+SLOTS = 512
+ROWS = 128
+PAGES = 64
+PAGE = 8
+GAIN = 512.0
+FLOPS = 4 * 2 * 512 * ROWS * SLOTS
+
+DAMP_LOG = -2.0
+UNDAMP = math.exp(2.0)
+STORE_WIDTHS = (256, 512, 512, 512, 256)
+
+
+def tile_attend_hvpagethensecond_s_kernel(
+    tc, query, query2, keys_words, keys_scales, gout, vals_words, vals_scales, dquery, base, offs, out
+):
+    nc = tc.nc
+    with ExitStack() as ctx:
+        held = ctx.enter_context(tc.tile_pool(name="held", bufs=1))
+        psum = ctx.enter_context(tc.psum_pool(name="psum", bufs=1))
+
+        def sbuf(name, shape, dtype, tag=None):
+            return held.tile(shape, dtype, name=name, tag=tag or name, align_bytes=64)
+
+        offsets = held.tile([P, SLOTS // 16], U16, name="offsets")
+        nc.sync.dma_start(offsets[:], offs)
+
+        def load_scales(name, scales):
+            pool_scales = sbuf(name, [P, POOL], U8)
+            nc.vector.memset(pool_scales[:].bitcast(I32), 0)
+            for r in range(4):
+                nc.scalar.dma_start(pool_scales[r:P:32, :].bitcast(I32), scales[0, r:16:4, :].bitcast(I32))
+            return pool_scales
+
+        def load_words(name, words, queue):
+            pool_words = sbuf(name, [P, POOL], U16)
+            queue.dma_start(pool_words[:].bitcast(I32), words[0].bitcast(I32))
+            return pool_words
+
+        def load_rows(raw, rows):
+            nc.sync.dma_start(raw, rows.rearrange("(p j) q -> p j q", j=PACK))
+
+        key_scales = load_scales("key_scales", keys_scales)
+        key_words = load_words("key_words", keys_words, nc.sync)
+        raw_q2 = sbuf("raw_q2", [P, PACK, ROWS], F32)
+        load_rows(raw_q2[:], query2)
+        raw_q = sbuf("raw_q", [P, PACK, ROWS], F32)
+        load_rows(raw_q[:], query)
+
+        half_log_a = sbuf("half_log_a", [P, 1], F32, "val_words")
+        nc.vector.memset(half_log_a[:], DAMP_LOG / 2)
+        half_log_b = sbuf("half_log_b", [P, 1], F32, "raw_late")
+        nc.vector.memset(half_log_b[:], DAMP_LOG / 2)
+        unit = sbuf("unit", [P, 1], F32, "result")
+        nc.vector.memset(unit[:], 1.0)
+        damp = sbuf("damp", [P, 1], F32)
+        nc.scalar.activation(damp[:], half_log_a[:], ACT.Exp, bias=half_log_b[:], scale=unit[:])
+
+        val_words = load_words("val_words", vals_words, nc.sync)
+        raw_late = sbuf("raw_late", [P, 2, PACK, ROWS], F32)
+        load_rows(raw_late[:, 0], dquery)
+        load_rows(raw_late[:, 1], gout)
+        result = sbuf("result", [P, POOL], F32)
+        nc.sync.dma_start(result[:], base)
+        placed = sbuf("placed", [P, POOL], F32)
+        nc.vector.memset(placed[:], 0.0)
+        val_scales = load_scales("val_scales", vals_scales)
+
+        def gather(name, window, dtype):
+            picked = sbuf(name, [P, SLOTS], dtype)
+            nc.vector.tensor_copy(picked[:], window[:].indirect(offsets[:]))
+            return picked
+
+        def interleave(name, raw):
+            grouped = sbuf(name, [P, ROWS, PACK], BF16)
+            nc.scalar.copy(grouped[:], raw.rearrange("p j q -> p q j"))
+            return grouped
+
+        def quantise(name, grouped):
+            codes = sbuf(name + "_codes", [P, ROWS], U32)
+            scales = sbuf(name + "_scales", [P, ROWS], U8)
+            nc.vector.quantize_mx(codes[:].bitcast(FP8X4), scales[:], grouped[:].rearrange("p q j -> p (q j)"))
+            return codes, scales
+
+        def product(name, rows, words, scales):
+            bank = psum.tile([P, SLOTS], F32, name=name)
+            nc.tensor.matmul_mx(
+                bank[:], lhsT=rows[0][:].bitcast(FP8X4), lhsT_scale=rows[1][:],
+                rhs=words[:].bitcast(FP4X4), rhs_scale=scales[:], start=True, stop=True,
+            )
+            return bank
+
+        def paged(ap):
+            return ap.rearrange("p (g j) -> p g j", j=PAGE)
+
+        def spread(ap):
+            return ap.unsqueeze(2).to_broadcast([P, PAGES, PAGE])
+
+        ks = gather("ks", key_scales, U8)
+        kw = gather("kw", key_words, U16)
+        grouped_q2 = interleave("grouped_q2", raw_q2[:])
+        grouped_q = interleave("grouped_q", raw_q[:])
+        mx_q2 = quantise("mx_q2", grouped_q2)
+        mx_q = quantise("mx_q", grouped_q)
+        b = product("b", mx_q2, kw, ks)
+        a = product("a", mx_q, kw, ks)
+        vs = gather("vs", val_scales, U8)
+        grouped_dq = interleave("grouped_dq", raw_late[:, 0])
+        grouped_g = interleave("grouped_g", raw_late[:, 1])
+
+        damped = sbuf("damped", [P, SLOTS], F32)
+        damped_sum = sbuf("damped_sum", [P, 1], F32)
+        nc.scalar.activation(damped[:], a[:], ACT.Exp, scale=damp[:], accum_out=damped_sum[:])
+        neg_shift = sbuf("neg_shift", [P, 1], F32)
+        nc.scalar.activation(
+            neg_shift[:], damped_sum[:].bitcast(U32), ACT.Copy,
+            scale=-UNDAMP * math.log(2.0) / 2.0**23, bias=UNDAMP * math.log(2.0) * 127.0,
+        )
+        pa = sbuf("pa", [P, SLOTS], F32)
+        z = sbuf("z", [P, 1], F32)
+        nc.scalar.activation(pa[:], a[:], ACT.Exp, bias=neg_shift[:], accum_out=z[:])
+
+        b_max = sbuf("b_max", [P, PAGES], F32)
+        nc.vector.tensor_reduce(b_max[:], paged(b[:]), AX.X, ALU.max)
+        mx_dq = quantise("mx_dq", grouped_dq)
+        mx_g = quantise("mx_g", grouped_g)
+        b_shifted = sbuf("b_shifted", [P, SLOTS], F32)
+        nc.vector.tensor_tensor(paged(b_shifted[:]), paged(b[:]), spread(b_max[:]), ALU.subtract)
+        pb = sbuf("pb", [P, SLOTS], F32)
+        nc.scalar.activation(pb[:], b_shifted[:], ACT.Exp)
+        ta = product("ta", mx_dq, kw, ks)
+        vw = gather("vw", val_words, U16)
+        c0 = product("c0", mx_g, vw, vs)
+
+        z_inv = sbuf("z_inv", [P, 1], F32)
+        nc.vector.reciprocal(z_inv[:], z[:])
+        sb = sbuf("sb", [P, PAGES], F32)
+        nc.vector.tensor_reduce(sb[:], paged(pb[:]), AX.X, ALU.add)
+        tp = sbuf("tp", [P, SLOTS], F32)
+        t_mean = sbuf("t_mean", [P, 1], F32)
+        nc.vector.scalar_tensor_tensor(tp[:], ta[:], z_inv[:], pa[:], ALU.mult, ALU.mult, accum_out=t_mean[:])
+        sb_inv = sbuf("sb_inv", [P, PAGES], F32)
+        nc.vector.reciprocal(sb_inv[:], sb[:])
+        drr = sbuf("drr", [P, SLOTS], F32)
+        nc.vector.scalar_tensor_tensor(drr[:], c0[:], z_inv[:], pb[:], ALU.mult, ALU.mult)
+        x = sbuf("x", [P, SLOTS], F32)
+        nc.vector.scalar_tensor_tensor(x[:], ta[:], t_mean[:], pa[:], ALU.subtract, ALU.mult)
+        sums = sbuf("sums", [P, 2, PAGES], F32)
+        nc.vector.tensor_reduce(sums[:, 0, :], paged(pa[:]), AX.X, ALU.add)
+        nc.vector.tensor_reduce(sums[:, 1, :], paged(x[:]), AX.X, ALU.add)
+        dr = sbuf("dr", [P, PAGES], F32)
+        nc.vector.tensor_reduce(dr[:], paged(drr[:]), AX.X, ALU.add)
+        weights = sbuf("weights", [P, 2, PAGES], F32)
+        nc.vector.scalar_tensor_tensor(
+            weights[:], sums[:], z_inv[:], sb_inv[:].unsqueeze(1).to_broadcast([P, 2, PAGES]), ALU.mult, ALU.mult
+        )
+        u = sbuf("u", [P, PAGES], F32)
+        nc.vector.scalar_tensor_tensor(u[:], dr[:], GAIN, sb_inv[:], ALU.mult, ALU.mult)
+        terms = sbuf("terms", [P, 2, PAGES], F32)
+        offset_c = sbuf("offset_c", [P, 1], F32)
+        u_mean = sbuf("u_mean", [P, 1], F32)
+        nc.vector.scalar_tensor_tensor(
+            terms[:, 1, :], dr[:], -GAIN, weights[:, 1, :], ALU.mult, ALU.mult, accum_out=offset_c[:]
+        )
+        nc.vector.scalar_tensor_tensor(
+            terms[:, 0, :], dr[:], GAIN, weights[:, 0, :], ALU.mult, ALU.mult, accum_out=u_mean[:]
+        )
+        along_pa = sbuf("along_pa", [P, SLOTS], F32)
+        nc.scalar.activation(along_pa[:], pa[:], ACT.Copy, scale=offset_c[:])
+        along_x = sbuf("along_x", [P, SLOTS], F32)
+        nc.vector.scalar_tensor_tensor(
+            paged(along_x[:]), spread(u[:]), u_mean[:], paged(x[:]), ALU.subtract, ALU.mult
+        )
+        nc.vector.tensor_tensor(placed[:].indirect(offsets[:]), along_x[:], along_pa[:], ALU.add)
+
+        start = 0
+        for n, width in enumerate(STORE_WIDTHS):
+            cols = slice(start, start + width)
+            nc.vector.tensor_tensor(result[:, cols], result[:, cols], placed[:, cols], ALU.add)
+            queue = nc.sync if n % 2 == 0 else nc.scalar
+            queue.dma_start(out[:, cols], result[:, cols])
+            start += width

@@ -2,6 +2,7 @@ import math
 from contextlib import ExitStack
 
 import concourse.mybir as mybir
+from concourse.masks import make_identity
 
 F32 = mybir.dt.float32
 BF16 = mybir.dt.bfloat16
@@ -27,6 +28,7 @@ FLOPS = 4 * 2 * 512 * ROWS * SLOTS
 
 DAMP_LOG = -2.0
 UNDAMP = math.exp(2.0)
+RAW_BYTES = PACK * ROWS * 4
 STORE_WIDTHS = (256, 512, 512, 512, 256)
 
 
@@ -36,6 +38,7 @@ def tile_attend_hvpagethensecond_s_kernel(
     nc = tc.nc
     with ExitStack() as ctx:
         held = ctx.enter_context(tc.tile_pool(name="held", bufs=1))
+        shared = ctx.enter_context(tc.tile_pool(name="shared", bufs=1))
         psum = ctx.enter_context(tc.psum_pool(name="psum", bufs=1))
 
         def sbuf(name, shape, dtype, tag=None):
@@ -44,11 +47,11 @@ def tile_attend_hvpagethensecond_s_kernel(
         offsets = held.tile([P, SLOTS // 16], U16, name="offsets")
         nc.sync.dma_start(offsets[:], offs)
 
-        def load_scales(name, scales):
+        def load_scales(name, scales, queue, engine):
             pool_scales = sbuf(name, [P, POOL], U8)
-            nc.vector.memset(pool_scales[:].bitcast(I32), 0)
+            engine.memset(pool_scales[:].bitcast(I32), 0)
             for r in range(4):
-                nc.scalar.dma_start(pool_scales[r:P:32, :].bitcast(I32), scales[0, r:16:4, :].bitcast(I32))
+                queue.dma_start(pool_scales[r:P:32, :].bitcast(I32), scales[0, r:16:4, :].bitcast(I32))
             return pool_scales
 
         def load_words(name, words, queue):
@@ -56,42 +59,48 @@ def tile_attend_hvpagethensecond_s_kernel(
             queue.dma_start(pool_words[:].bitcast(I32), words[0].bitcast(I32))
             return pool_words
 
-        def load_rows(raw, rows):
-            nc.sync.dma_start(raw, rows.rearrange("(p j) q -> p j q", j=PACK))
+        def load_rows(raw, rows, queue):
+            queue.dma_start(raw, rows.rearrange("(p j) q -> p j q", j=PACK))
 
-        key_scales = load_scales("key_scales", keys_scales)
         key_words = load_words("key_words", keys_words, nc.sync)
-        raw_q2 = sbuf("raw_q2", [P, PACK, ROWS], F32)
-        load_rows(raw_q2[:], query2)
-        raw_q = sbuf("raw_q", [P, PACK, ROWS], F32)
-        load_rows(raw_q[:], query)
+        key_scales = load_scales("key_scales", keys_scales, nc.sync, nc.vector)
 
-        half_log_a = sbuf("half_log_a", [P, 1], F32, "val_words")
-        nc.vector.memset(half_log_a[:], DAMP_LOG / 2)
-        half_log_b = sbuf("half_log_b", [P, 1], F32, "raw_late")
-        nc.vector.memset(half_log_b[:], DAMP_LOG / 2)
-        unit = sbuf("unit", [P, 1], F32, "result")
-        nc.vector.memset(unit[:], 1.0)
+        def column(name, value, tag):
+            tile = sbuf(name, [P, 1], F32, tag)
+            nc.vector.memset(tile[:], value)
+            return tile
+
+        first_half = column("first_half", DAMP_LOG / 2, "raw_q")
+        second_half = column("second_half", DAMP_LOG / 2, "raw_q2")
+        damp_log = sbuf("damp_log", [P, 1], F32, "val_words")
+        nc.vector.tensor_tensor(damp_log[:], first_half[:], second_half[:], ALU.add)
+        raw_q = sbuf("raw_q", [P, PACK, ROWS], F32)
+        load_rows(raw_q[:], query, nc.sync)
+        raw_q2 = sbuf("raw_q2", [P, PACK, ROWS], F32)
+        load_rows(raw_q2[:], query2, nc.sync)
+
+        no_bias = shared.tile([P, 16], F32, name="no_bias", offset=RAW_BYTES - 32)
+        nc.vector.memset(no_bias[:], 0.0)
+        unit_b = column("unit_b", 1.0, "val_scales")
         damp = sbuf("damp", [P, 1], F32)
-        nc.scalar.activation(damp[:], half_log_a[:], ACT.Exp, bias=half_log_b[:], scale=unit[:])
+        nc.scalar.activation(damp[:], damp_log[:], ACT.Exp, bias=no_bias[:, 0:1], scale=unit_b[:])
+        identity = sbuf("identity", [P, P], F32)
+        make_identity(nc, identity[:])
 
         val_words = load_words("val_words", vals_words, nc.sync)
-        raw_late = sbuf("raw_late", [P, 2, PACK, ROWS], F32)
-        load_rows(raw_late[:, 0], dquery)
-        load_rows(raw_late[:, 1], gout)
-        result = sbuf("result", [P, POOL], F32)
-        nc.sync.dma_start(result[:], base)
-        placed = sbuf("placed", [P, POOL], F32)
-        nc.vector.memset(placed[:], 0.0)
-        val_scales = load_scales("val_scales", vals_scales)
+        raw_dq = shared.tile([P, PACK, ROWS], F32, name="raw_dq", offset=0)
+        load_rows(raw_dq[:], dquery, nc.sync)
+        raw_g = shared.tile([P, PACK, ROWS], F32, name="raw_g", offset=RAW_BYTES)
+        load_rows(raw_g[:], gout, nc.sync)
+        val_scales = load_scales("val_scales", vals_scales, nc.sync, nc.vector)
 
-        def gather(name, window, dtype):
-            picked = sbuf(name, [P, SLOTS], dtype)
+        def gather(name, window, dtype, tag=None):
+            picked = sbuf(name, [P, SLOTS], dtype, tag)
             nc.vector.tensor_copy(picked[:], window[:].indirect(offsets[:]))
             return picked
 
-        def interleave(name, raw):
-            grouped = sbuf(name, [P, ROWS, PACK], BF16)
+        def interleave(name, raw, tag=None):
+            grouped = sbuf(name, [P, ROWS, PACK], BF16, tag)
             nc.scalar.copy(grouped[:], raw.rearrange("p j q -> p q j"))
             return grouped
 
@@ -115,19 +124,45 @@ def tile_attend_hvpagethensecond_s_kernel(
         def spread(ap):
             return ap.unsqueeze(2).to_broadcast([P, PAGES, PAGE])
 
-        ks = gather("ks", key_scales, U8)
-        kw = gather("kw", key_words, U16)
-        grouped_q2 = interleave("grouped_q2", raw_q2[:])
-        grouped_q = interleave("grouped_q", raw_q[:])
-        mx_q2 = quantise("mx_q2", grouped_q2)
-        mx_q = quantise("mx_q", grouped_q)
-        b = product("b", mx_q2, kw, ks)
-        a = product("a", mx_q, kw, ks)
-        vs = gather("vs", val_scales, U8)
-        grouped_dq = interleave("grouped_dq", raw_late[:, 0])
-        grouped_g = interleave("grouped_g", raw_late[:, 1])
+        def quad_sums(name, arrays):
+            count = len(arrays)
+            turned = psum.tile([P, count, P], F32, name=name + "_turned")
+            for n, array in enumerate(arrays):
+                for j in range(4):
+                    nc.tensor.matmul(
+                        turned[:, n, :], lhsT=array[:, j:SLOTS:4], rhs=identity[:],
+                        is_transpose=True, start=(j == 0), stop=(j == 3),
+                    )
+            staged = sbuf(name + "_staged", [P, count, P], F32)
+            nc.scalar.copy(staged[:], turned[:])
+            sums = psum.tile([P, count, P], F32, name=name)
+            for n in range(count):
+                nc.tensor.transpose(sums[:, n, :], staged[:, n, :], identity[:])
+            return sums
 
-        damped = sbuf("damped", [P, SLOTS], F32)
+        def halves(ap):
+            return ap.rearrange("p (g h) -> p g h", h=2)
+
+        def spread2(ap):
+            return ap.unsqueeze(2).to_broadcast([P, PAGES, 2])
+
+        kw = gather("kw", key_words, U16)
+        ks = gather("ks", key_scales, U8)
+        grouped_q = interleave("grouped_q", raw_q[:])
+        grouped_q2 = interleave("grouped_q2", raw_q2[:])
+        mx_q = quantise("mx_q", grouped_q)
+        mx_q2 = quantise("mx_q2", grouped_q2)
+        placed = sbuf("placed", [P, POOL], F32, "grouped_q2")
+        nc.gpsimd.memset(placed[:], 0.0)
+        a = product("a", mx_q, kw, ks)
+        b = product("b", mx_q2, kw, ks)
+        vw = gather("vw", val_words, U16)
+        result = sbuf("result", [P, POOL], F32, "val_words")
+        nc.sync.dma_start(result[:], base)
+        vs = gather("vs", val_scales, U8)
+        grouped_dq = interleave("grouped_dq", raw_dq[:])
+
+        damped = shared.tile([P, SLOTS], F32, name="damped", offset=0)
         damped_sum = sbuf("damped_sum", [P, 1], F32)
         nc.scalar.activation(damped[:], a[:], ACT.Exp, scale=damp[:], accum_out=damped_sum[:])
         neg_shift = sbuf("neg_shift", [P, 1], F32)
@@ -139,51 +174,52 @@ def tile_attend_hvpagethensecond_s_kernel(
         z = sbuf("z", [P, 1], F32)
         nc.scalar.activation(pa[:], a[:], ACT.Exp, bias=neg_shift[:], accum_out=z[:])
 
-        b_max = sbuf("b_max", [P, PAGES], F32)
-        nc.vector.tensor_reduce(b_max[:], paged(b[:]), AX.X, ALU.max)
+        grouped_g = interleave("grouped_g", raw_g[:], "neg_shift")
         mx_dq = quantise("mx_dq", grouped_dq)
-        mx_g = quantise("mx_g", grouped_g)
-        b_shifted = sbuf("b_shifted", [P, SLOTS], F32)
-        nc.vector.tensor_tensor(paged(b_shifted[:]), paged(b[:]), spread(b_max[:]), ALU.subtract)
-        pb = sbuf("pb", [P, SLOTS], F32)
-        nc.scalar.activation(pb[:], b_shifted[:], ACT.Exp)
-        ta = product("ta", mx_dq, kw, ks)
-        vw = gather("vw", val_words, U16)
-        c0 = product("c0", mx_g, vw, vs)
-
+        b_max = sbuf("b_max", [P, PAGES], F32, "val_scales")
+        nc.vector.tensor_reduce(b_max[:], paged(b[:]), AX.X, ALU.max)
         z_inv = sbuf("z_inv", [P, 1], F32)
         nc.vector.reciprocal(z_inv[:], z[:])
-        sb = sbuf("sb", [P, PAGES], F32)
-        nc.vector.tensor_reduce(sb[:], paged(pb[:]), AX.X, ALU.add)
+        b_shifted = sbuf("b_shifted", [P, SLOTS], F32)
+        nc.vector.tensor_tensor(paged(b_shifted[:]), paged(b[:]), spread(b_max[:]), ALU.subtract)
+        pb = shared.tile([P, SLOTS], F32, name="pb", offset=RAW_BYTES)
+        nc.scalar.activation(pb[:], b_shifted[:], ACT.Exp)
+        ta = product("ta", mx_dq, kw, ks)
+
+        gain = sbuf("gain", [P, 1], F32)
+        nc.scalar.activation(gain[:], z_inv[:], ACT.Copy, scale=GAIN)
+        p_sums = quad_sums("p_sums", [pa])
         tp = sbuf("tp", [P, SLOTS], F32)
         t_mean = sbuf("t_mean", [P, 1], F32)
         nc.vector.scalar_tensor_tensor(tp[:], ta[:], z_inv[:], pa[:], ALU.mult, ALU.mult, accum_out=t_mean[:])
-        sb_inv = sbuf("sb_inv", [P, PAGES], F32)
-        nc.vector.reciprocal(sb_inv[:], sb[:])
-        drr = sbuf("drr", [P, SLOTS], F32)
-        nc.vector.scalar_tensor_tensor(drr[:], c0[:], z_inv[:], pb[:], ALU.mult, ALU.mult)
+        mx_g = quantise("mx_g", grouped_g)
+        c0 = product("c0", mx_g, vw, vs)
+        tp_sums = quad_sums("tp_sums", [tp])
         x = sbuf("x", [P, SLOTS], F32)
         nc.vector.scalar_tensor_tensor(x[:], ta[:], t_mean[:], pa[:], ALU.subtract, ALU.mult)
-        sums = sbuf("sums", [P, 2, PAGES], F32)
-        nc.vector.tensor_reduce(sums[:, 0, :], paged(pa[:]), AX.X, ALU.add)
-        nc.vector.tensor_reduce(sums[:, 1, :], paged(x[:]), AX.X, ALU.add)
+        sb = sbuf("sb", [P, PAGES], F32)
+        nc.vector.tensor_reduce(sb[:], paged(pb[:]), AX.X, ALU.add)
+        drr = sbuf("drr", [P, SLOTS], F32)
+        nc.vector.scalar_tensor_tensor(drr[:], c0[:], gain[:], pb[:], ALU.mult, ALU.mult)
+        sb_inv = sbuf("sb_inv", [P, PAGES], F32)
+        nc.vector.reciprocal(sb_inv[:], sb[:])
         dr = sbuf("dr", [P, PAGES], F32)
         nc.vector.tensor_reduce(dr[:], paged(drr[:]), AX.X, ALU.add)
-        weights = sbuf("weights", [P, 2, PAGES], F32)
-        nc.vector.scalar_tensor_tensor(
-            weights[:], sums[:], z_inv[:], sb_inv[:].unsqueeze(1).to_broadcast([P, 2, PAGES]), ALU.mult, ALU.mult
-        )
         u = sbuf("u", [P, PAGES], F32)
-        nc.vector.scalar_tensor_tensor(u[:], dr[:], GAIN, sb_inv[:], ALU.mult, ALU.mult)
-        terms = sbuf("terms", [P, 2, PAGES], F32)
-        offset_c = sbuf("offset_c", [P, 1], F32)
+        nc.vector.tensor_tensor(u[:], dr[:], sb_inv[:], ALU.mult)
+        terms = sbuf("terms", [P, 2, P], F32)
         u_mean = sbuf("u_mean", [P, 1], F32)
+        neg_v = sbuf("neg_v", [P, 1], F32)
         nc.vector.scalar_tensor_tensor(
-            terms[:, 1, :], dr[:], -GAIN, weights[:, 1, :], ALU.mult, ALU.mult, accum_out=offset_c[:]
+            halves(terms[:, 0, :]), halves(p_sums[:, 0, :]), z_inv[:], spread2(u[:]), ALU.mult, ALU.mult,
+            accum_out=u_mean[:],
         )
         nc.vector.scalar_tensor_tensor(
-            terms[:, 0, :], dr[:], GAIN, weights[:, 0, :], ALU.mult, ALU.mult, accum_out=u_mean[:]
+            halves(terms[:, 1, :]), halves(tp_sums[:, 0, :]), -1.0, spread2(u[:]), ALU.mult, ALU.mult,
+            accum_out=neg_v[:],
         )
+        offset_c = sbuf("offset_c", [P, 1], F32)
+        nc.scalar.activation(offset_c[:], u_mean[:], ACT.Identity, scale=t_mean[:], bias=neg_v[:])
         along_pa = sbuf("along_pa", [P, SLOTS], F32)
         nc.scalar.activation(along_pa[:], pa[:], ACT.Copy, scale=offset_c[:])
         along_x = sbuf("along_x", [P, SLOTS], F32)

@@ -28,7 +28,6 @@ FLOPS = 4 * 2 * 512 * ROWS * SLOTS
 
 DAMP_LOG = -2.0
 UNDAMP = math.exp(2.0)
-RAW_BYTES = PACK * ROWS * 4
 STORE_WIDTHS = (256, 512, 512, 512, 256)
 
 
@@ -38,7 +37,6 @@ def tile_attend_hvpagethensecond_s_kernel(
     nc = tc.nc
     with ExitStack() as ctx:
         held = ctx.enter_context(tc.tile_pool(name="held", bufs=1))
-        shared = ctx.enter_context(tc.tile_pool(name="shared", bufs=1))
         psum = ctx.enter_context(tc.psum_pool(name="psum", bufs=1))
 
         def sbuf(name, shape, dtype, tag=None):
@@ -47,9 +45,9 @@ def tile_attend_hvpagethensecond_s_kernel(
         offsets = held.tile([P, SLOTS // 16], U16, name="offsets")
         nc.sync.dma_start(offsets[:], offs)
 
-        def load_scales(name, scales, queue, engine):
+        def load_scales(name, scales, queue):
             pool_scales = sbuf(name, [P, POOL], U8)
-            engine.memset(pool_scales[:].bitcast(I32), 0)
+            nc.vector.memset(pool_scales[:].bitcast(I32), 0)
             for r in range(4):
                 queue.dma_start(pool_scales[r:P:32, :].bitcast(I32), scales[0, r:16:4, :].bitcast(I32))
             return pool_scales
@@ -63,7 +61,7 @@ def tile_attend_hvpagethensecond_s_kernel(
             queue.dma_start(raw, rows.rearrange("(p j) q -> p j q", j=PACK))
 
         key_words = load_words("key_words", keys_words, nc.sync)
-        key_scales = load_scales("key_scales", keys_scales, nc.sync, nc.vector)
+        key_scales = load_scales("key_scales", keys_scales, nc.sync)
 
         def column(name, value, tag):
             tile = sbuf(name, [P, 1], F32, tag)
@@ -72,27 +70,28 @@ def tile_attend_hvpagethensecond_s_kernel(
 
         first_half = column("first_half", DAMP_LOG / 2, "raw_q")
         second_half = column("second_half", DAMP_LOG / 2, "raw_q2")
+        unit_a = column("unit_a", 1.0, "placed")
         damp_log = sbuf("damp_log", [P, 1], F32, "val_words")
-        nc.vector.tensor_tensor(damp_log[:], first_half[:], second_half[:], ALU.add)
+        nc.vector.scalar_tensor_tensor(damp_log[:], first_half[:], unit_a[:], second_half[:], ALU.mult, ALU.add)
         raw_q = sbuf("raw_q", [P, PACK, ROWS], F32)
         load_rows(raw_q[:], query, nc.sync)
         raw_q2 = sbuf("raw_q2", [P, PACK, ROWS], F32)
         load_rows(raw_q2[:], query2, nc.sync)
 
-        no_bias = shared.tile([P, 16], F32, name="no_bias", offset=RAW_BYTES - 32)
-        nc.vector.memset(no_bias[:], 0.0)
+        no_bias = column("no_bias", 0.0, "raw_late")
         unit_b = column("unit_b", 1.0, "val_scales")
         damp = sbuf("damp", [P, 1], F32)
-        nc.scalar.activation(damp[:], damp_log[:], ACT.Exp, bias=no_bias[:, 0:1], scale=unit_b[:])
+        nc.scalar.activation(damp[:], damp_log[:], ACT.Exp, bias=no_bias[:], scale=unit_b[:])
         identity = sbuf("identity", [P, P], F32)
         make_identity(nc, identity[:])
 
         val_words = load_words("val_words", vals_words, nc.sync)
-        raw_dq = shared.tile([P, PACK, ROWS], F32, name="raw_dq", offset=0)
-        load_rows(raw_dq[:], dquery, nc.sync)
-        raw_g = shared.tile([P, PACK, ROWS], F32, name="raw_g", offset=RAW_BYTES)
-        load_rows(raw_g[:], gout, nc.sync)
-        val_scales = load_scales("val_scales", vals_scales, nc.sync, nc.vector)
+        raw_late = sbuf("raw_late", [P, 2, PACK, ROWS], F32)
+        load_rows(raw_late[:, 0], dquery, nc.sync)
+        load_rows(raw_late[:, 1], gout, nc.sync)
+        val_scales = load_scales("val_scales", vals_scales, nc.sync)
+        placed = sbuf("placed", [P, POOL], F32)
+        nc.vector.memset(placed[:], 0.0)
 
         def gather(name, window, dtype, tag=None):
             picked = sbuf(name, [P, SLOTS], dtype, tag)
@@ -108,12 +107,12 @@ def tile_attend_hvpagethensecond_s_kernel(
             codes = sbuf(name + "_codes", [P, ROWS], U32)
             scales = sbuf(name + "_scales", [P, ROWS], U8)
             nc.vector.quantize_mx(codes[:].bitcast(FP8X4), scales[:], grouped[:].rearrange("p q j -> p (q j)"))
-            return codes, scales
+            return codes[:], scales[:]
 
         def product(name, rows, words, scales):
             bank = psum.tile([P, SLOTS], F32, name=name)
             nc.tensor.matmul_mx(
-                bank[:], lhsT=rows[0][:].bitcast(FP8X4), lhsT_scale=rows[1][:],
+                bank[:], lhsT=rows[0].bitcast(FP8X4), lhsT_scale=rows[1],
                 rhs=words[:].bitcast(FP4X4), rhs_scale=scales[:], start=True, stop=True,
             )
             return bank
@@ -148,21 +147,19 @@ def tile_attend_hvpagethensecond_s_kernel(
 
         kw = gather("kw", key_words, U16)
         ks = gather("ks", key_scales, U8)
+        result = sbuf("result", [P, POOL], F32, "key_words")
+        nc.sync.dma_start(result[:], base)
         grouped_q = interleave("grouped_q", raw_q[:])
         grouped_q2 = interleave("grouped_q2", raw_q2[:])
         mx_q = quantise("mx_q", grouped_q)
         mx_q2 = quantise("mx_q2", grouped_q2)
-        placed = sbuf("placed", [P, POOL], F32, "grouped_q2")
-        nc.gpsimd.memset(placed[:], 0.0)
         a = product("a", mx_q, kw, ks)
         b = product("b", mx_q2, kw, ks)
         vw = gather("vw", val_words, U16)
-        result = sbuf("result", [P, POOL], F32, "val_words")
-        nc.sync.dma_start(result[:], base)
-        vs = gather("vs", val_scales, U8)
-        grouped_dq = interleave("grouped_dq", raw_dq[:])
+        grouped_late = sbuf("grouped_late", [P, 2, ROWS, PACK], BF16)
+        nc.scalar.copy(grouped_late[:], raw_late[:].rearrange("p o j q -> p o q j"))
 
-        damped = shared.tile([P, SLOTS], F32, name="damped", offset=0)
+        damped = sbuf("damped", [P, SLOTS], F32, "raw_late")
         damped_sum = sbuf("damped_sum", [P, 1], F32)
         nc.scalar.activation(damped[:], a[:], ACT.Exp, scale=damp[:], accum_out=damped_sum[:])
         neg_shift = sbuf("neg_shift", [P, 1], F32)
@@ -174,52 +171,58 @@ def tile_attend_hvpagethensecond_s_kernel(
         z = sbuf("z", [P, 1], F32)
         nc.scalar.activation(pa[:], a[:], ACT.Exp, bias=neg_shift[:], accum_out=z[:])
 
-        grouped_g = interleave("grouped_g", raw_g[:], "neg_shift")
-        mx_dq = quantise("mx_dq", grouped_dq)
-        b_max = sbuf("b_max", [P, PAGES], F32, "val_scales")
+        b_max = sbuf("b_max", [P, PAGES], F32, "val_words")
         nc.vector.tensor_reduce(b_max[:], paged(b[:]), AX.X, ALU.max)
-        z_inv = sbuf("z_inv", [P, 1], F32)
-        nc.vector.reciprocal(z_inv[:], z[:])
+        late_codes = sbuf("late_codes", [P, 2 * ROWS], U32)
+        late_scales = sbuf("late_scales", [P, 2 * ROWS], U8)
+        nc.vector.quantize_mx(
+            late_codes[:].bitcast(FP8X4), late_scales[:], grouped_late[:].rearrange("p o q j -> p (o q j)")
+        )
+        mx_dq = (late_codes[:, :ROWS], late_scales[:, :ROWS])
+        mx_g = (late_codes[:, ROWS:], late_scales[:, ROWS:])
         b_shifted = sbuf("b_shifted", [P, SLOTS], F32)
         nc.vector.tensor_tensor(paged(b_shifted[:]), paged(b[:]), spread(b_max[:]), ALU.subtract)
-        pb = shared.tile([P, SLOTS], F32, name="pb", offset=RAW_BYTES)
+        pb = sbuf("pb", [P, SLOTS], F32, "neg_shift")
         nc.scalar.activation(pb[:], b_shifted[:], ACT.Exp)
         ta = product("ta", mx_dq, kw, ks)
+        vs = gather("vs", val_scales, U8, "val_words")
+        c0 = product("c0", mx_g, vw, vs)
 
+        z_inv = sbuf("z_inv", [P, 1], F32, "val_scales")
+        nc.vector.reciprocal(z_inv[:], z[:])
         gain = sbuf("gain", [P, 1], F32)
         nc.scalar.activation(gain[:], z_inv[:], ACT.Copy, scale=GAIN)
+        neg_z_inv = sbuf("neg_z_inv", [P, 1], F32)
+        nc.scalar.activation(neg_z_inv[:], z_inv[:], ACT.Copy, scale=-1.0)
         p_sums = quad_sums("p_sums", [pa])
         tp = sbuf("tp", [P, SLOTS], F32)
         t_mean = sbuf("t_mean", [P, 1], F32)
         nc.vector.scalar_tensor_tensor(tp[:], ta[:], z_inv[:], pa[:], ALU.mult, ALU.mult, accum_out=t_mean[:])
-        mx_g = quantise("mx_g", grouped_g)
-        c0 = product("c0", mx_g, vw, vs)
-        tp_sums = quad_sums("tp_sums", [tp])
-        x = sbuf("x", [P, SLOTS], F32)
-        nc.vector.scalar_tensor_tensor(x[:], ta[:], t_mean[:], pa[:], ALU.subtract, ALU.mult)
         sb = sbuf("sb", [P, PAGES], F32)
         nc.vector.tensor_reduce(sb[:], paged(pb[:]), AX.X, ALU.add)
+        x = sbuf("x", [P, SLOTS], F32)
+        nc.vector.scalar_tensor_tensor(x[:], ta[:], t_mean[:], pa[:], ALU.subtract, ALU.mult)
         drr = sbuf("drr", [P, SLOTS], F32)
         nc.vector.scalar_tensor_tensor(drr[:], c0[:], gain[:], pb[:], ALU.mult, ALU.mult)
         sb_inv = sbuf("sb_inv", [P, PAGES], F32)
         nc.vector.reciprocal(sb_inv[:], sb[:])
         dr = sbuf("dr", [P, PAGES], F32)
         nc.vector.tensor_reduce(dr[:], paged(drr[:]), AX.X, ALU.add)
+        xs = sbuf("xs", [P, PAGES], F32)
+        nc.vector.tensor_reduce(xs[:], paged(x[:]), AX.X, ALU.add)
         u = sbuf("u", [P, PAGES], F32)
         nc.vector.tensor_tensor(u[:], dr[:], sb_inv[:], ALU.mult)
-        terms = sbuf("terms", [P, 2, P], F32)
-        u_mean = sbuf("u_mean", [P, 1], F32)
-        neg_v = sbuf("neg_v", [P, 1], F32)
+        c_terms = sbuf("c_terms", [P, PAGES], F32)
+        offset_c = sbuf("offset_c", [P, 1], F32)
         nc.vector.scalar_tensor_tensor(
-            halves(terms[:, 0, :]), halves(p_sums[:, 0, :]), z_inv[:], spread2(u[:]), ALU.mult, ALU.mult,
+            c_terms[:], xs[:], neg_z_inv[:], u[:], ALU.mult, ALU.mult, accum_out=offset_c[:]
+        )
+        u_terms = sbuf("u_terms", [P, P], F32)
+        u_mean = sbuf("u_mean", [P, 1], F32)
+        nc.vector.scalar_tensor_tensor(
+            halves(u_terms[:]), halves(p_sums[:, 0, :]), z_inv[:], spread2(u[:]), ALU.mult, ALU.mult,
             accum_out=u_mean[:],
         )
-        nc.vector.scalar_tensor_tensor(
-            halves(terms[:, 1, :]), halves(tp_sums[:, 0, :]), -1.0, spread2(u[:]), ALU.mult, ALU.mult,
-            accum_out=neg_v[:],
-        )
-        offset_c = sbuf("offset_c", [P, 1], F32)
-        nc.scalar.activation(offset_c[:], u_mean[:], ACT.Identity, scale=t_mean[:], bias=neg_v[:])
         along_pa = sbuf("along_pa", [P, SLOTS], F32)
         nc.scalar.activation(along_pa[:], pa[:], ACT.Copy, scale=offset_c[:])
         along_x = sbuf("along_x", [P, SLOTS], F32)

@@ -171,8 +171,9 @@ def tile_attend_hvpagethensecond_s_kernel(
         z = sbuf("z", [P, 1], F32)
         nc.scalar.activation(pa[:], a[:], ACT.Exp, bias=neg_shift[:], accum_out=z[:])
 
-        b_max = sbuf("b_max", [P, PAGES], F32, "val_words")
+        b_max = sbuf("b_max", [P, PAGES], F32)
         nc.vector.tensor_reduce(b_max[:], paged(b[:]), AX.X, ALU.max)
+        vs = gather("vs", val_scales, U8)
         late_codes = sbuf("late_codes", [P, 2 * ROWS], U32)
         late_scales = sbuf("late_scales", [P, 2 * ROWS], U8)
         nc.vector.quantize_mx(
@@ -185,10 +186,9 @@ def tile_attend_hvpagethensecond_s_kernel(
         pb = sbuf("pb", [P, SLOTS], F32, "neg_shift")
         nc.scalar.activation(pb[:], b_shifted[:], ACT.Exp)
         ta = product("ta", mx_dq, kw, ks)
-        vs = gather("vs", val_scales, U8, "val_words")
         c0 = product("c0", mx_g, vw, vs)
 
-        z_inv = sbuf("z_inv", [P, 1], F32, "val_scales")
+        z_inv = sbuf("z_inv", [P, 1], F32)
         nc.vector.reciprocal(z_inv[:], z[:])
         gain = sbuf("gain", [P, 1], F32)
         nc.scalar.activation(gain[:], z_inv[:], ACT.Copy, scale=GAIN)
@@ -198,14 +198,16 @@ def tile_attend_hvpagethensecond_s_kernel(
         tp = sbuf("tp", [P, SLOTS], F32)
         t_mean = sbuf("t_mean", [P, 1], F32)
         nc.vector.scalar_tensor_tensor(tp[:], ta[:], z_inv[:], pa[:], ALU.mult, ALU.mult, accum_out=t_mean[:])
-        sb = sbuf("sb", [P, PAGES], F32)
-        nc.vector.tensor_reduce(sb[:], paged(pb[:]), AX.X, ALU.add)
         x = sbuf("x", [P, SLOTS], F32)
         nc.vector.scalar_tensor_tensor(x[:], ta[:], t_mean[:], pa[:], ALU.subtract, ALU.mult)
+        sb = sbuf("sb", [P, PAGES], F32)
+        nc.vector.tensor_reduce(sb[:], paged(pb[:]), AX.X, ALU.add)
         drr = sbuf("drr", [P, SLOTS], F32)
         nc.vector.scalar_tensor_tensor(drr[:], c0[:], gain[:], pb[:], ALU.mult, ALU.mult)
         sb_inv = sbuf("sb_inv", [P, PAGES], F32)
-        nc.vector.reciprocal(sb_inv[:], sb[:])
+        sb_rsqrt = sbuf("sb_rsqrt", [P, PAGES], F32)
+        nc.scalar.activation(sb_rsqrt[:], sb[:], ACT.Abs_reciprocal_sqrt)
+        nc.scalar.activation(sb_inv[:], sb_rsqrt[:], ACT.Square)
         dr = sbuf("dr", [P, PAGES], F32)
         nc.vector.tensor_reduce(dr[:], paged(drr[:]), AX.X, ALU.add)
         xs = sbuf("xs", [P, PAGES], F32)

import math
from contextlib import ExitStack

import concourse.mybir as mybir
from concourse.masks import make_identity

F32 = mybir.dt.float32
BF16 = mybir.dt.bfloat16
I32 = mybir.dt.int32
U32 = mybir.dt.uint32
U16 = mybir.dt.uint16
U8 = mybir.dt.uint8
FP8X4 = mybir.dt.float8_e4m3fn_x4
FP4X4 = mybir.dt.float4_e2m1fn_x4
ALU = mybir.AluOpType
ACT = mybir.ActivationFunctionType
AX = mybir.AxisListType

P = 128
PACK = 4
POOL = 2048
SLOTS = 512
ROWS = 128
PAGES = 64
PAGE = 8
GAIN = 512.0
FLOPS = 4 * 2 * 512 * ROWS * SLOTS

DAMP_LOG = -2.0
UNDAMP = math.exp(2.0)
STORE_WIDTHS = (256, 512, 512, 512, 256)


def tile_attend_hvpagethensecond_s_kernel(
    tc, query, query2, keys_words, keys_scales, gout, vals_words, vals_scales, dquery, base, offs, out
):
    nc = tc.nc
    with ExitStack() as ctx:
        held = ctx.enter_context(tc.tile_pool(name="held", bufs=1))
        psum = ctx.enter_context(tc.psum_pool(name="psum", bufs=1))

        def sbuf(name, shape, dtype, tag=None):
            return held.tile(shape, dtype, name=name, tag=tag or name, align_bytes=64)

        offsets = held.tile([P, SLOTS // 16], U16, name="offsets")
        nc.sync.dma_start(offsets[:], offs)

        def load_scales(name, scales, queue):
            pool_scales = sbuf(name, [P, POOL], U8)
            nc.vector.memset(pool_scales[:].bitcast(I32), 0)
            for r in range(4):
                queue.dma_start(pool_scales[r:P:32, :].bitcast(I32), scales[0, r:16:4, :].bitcast(I32))
            return pool_scales

        def load_words(name, words, queue):
            pool_words = sbuf(name, [P, POOL], U16)
            queue.dma_start(pool_words[:].bitcast(I32), words[0].bitcast(I32))
            return pool_words

        def load_rows(raw, rows, queue):
            queue.dma_start(raw, rows.rearrange("(p j) q -> p j q", j=PACK))

        key_words = load_words("key_words", keys_words, nc.sync)
        key_scales = load_scales("key_scales", keys_scales, nc.sync)

        def column(name, value, tag):
            tile = sbuf(name, [P, 1], F32, tag)
            nc.vector.memset(tile[:], value)
            return tile

        first_half = column("first_half", DAMP_LOG / 2, "raw_q")
        second_half = column("second_half", DAMP_LOG / 2, "raw_q2")
        unit_a = column("unit_a", 1.0, "placed")
        damp_log = sbuf("damp_log", [P, 1], F32, "val_words")
        nc.vector.scalar_tensor_tensor(damp_log[:], first_half[:], unit_a[:], second_half[:], ALU.mult, ALU.add)
        raw_q = sbuf("raw_q", [P, PACK, ROWS], F32)
        load_rows(raw_q[:], query, nc.sync)
        raw_q2 = sbuf("raw_q2", [P, PACK, ROWS], F32)
        load_rows(raw_q2[:], query2, nc.sync)

        no_bias = column("no_bias", 0.0, "raw_late")
        unit_b = column("unit_b", 1.0, "val_scales")
        damp = sbuf("damp", [P, 1], F32)
        nc.scalar.activation(damp[:], damp_log[:], ACT.Exp, bias=no_bias[:], scale=unit_b[:])
        identity = sbuf("identity", [P, P], F32)
        make_identity(nc, identity[:])

        val_words = load_words("val_words", vals_words, nc.sync)
        raw_late = sbuf("raw_late", [P, 2, PACK, ROWS], F32)
        load_rows(raw_late[:, 0], dquery, nc.sync)
        load_rows(raw_late[:, 1], gout, nc.sync)
        val_scales = load_scales("val_scales", vals_scales, nc.sync)
        placed = sbuf("placed", [P, POOL], F32)
        nc.vector.memset(placed[:], 0.0)

        def gather(name, window, dtype, tag=None):
            picked = sbuf(name, [P, SLOTS], dtype, tag)
            nc.vector.tensor_copy(picked[:], window[:].indirect(offsets[:]))
            return picked

        def interleave(name, raw, tag=None):
            grouped = sbuf(name, [P, ROWS, PACK], BF16, tag)
            nc.scalar.copy(grouped[:], raw.rearrange("p j q -> p q j"))
            return grouped

        def quantise(name, grouped):
            codes = sbuf(name + "_codes", [P, ROWS], U32)
            scales = sbuf(name + "_scales", [P, ROWS], U8)
            nc.vector.quantize_mx(codes[:].bitcast(FP8X4), scales[:], grouped[:].rearrange("p q j -> p (q j)"))
            return codes[:], scales[:]

        def product(name, rows, words, scales):
            bank = psum.tile([P, SLOTS], F32, name=name)
            nc.tensor.matmul_mx(
                bank[:], lhsT=rows[0].bitcast(FP8X4), lhsT_scale=rows[1],
                rhs=words[:].bitcast(FP4X4), rhs_scale=scales[:], start=True, stop=True,
            )
            return bank

        def paged(ap):
            return ap.rearrange("p (g j) -> p g j", j=PAGE)

        def spread(ap):
            return ap.unsqueeze(2).to_broadcast([P, PAGES, PAGE])

        def quad_sums(name, arrays):
            count = len(arrays)
            turned = psum.tile([P, count, P], F32, name=name + "_turned")
            for n, array in enumerate(arrays):
                for j in range(4):
                    nc.tensor.matmul(
                        turned[:, n, :], lhsT=array[:, j:SLOTS:4], rhs=identity[:],
                        is_transpose=True, start=(j == 0), stop=(j == 3),
                    )
            staged = sbuf(name + "_staged", [P, count, P], F32)
            nc.scalar.copy(staged[:], turned[:])
            sums = psum.tile([P, count, P], F32, name=name)
            for n in range(count):
                nc.tensor.transpose(sums[:, n, :], staged[:, n, :], identity[:])
            return sums

        def halves(ap):
            return ap.rearrange("p (g h) -> p g h", h=2)

        def spread2(ap):
            return ap.unsqueeze(2).to_broadcast([P, PAGES, 2])

        kw = gather("kw", key_words, U16)
        ks = gather("ks", key_scales, U8)
        result = sbuf("result", [P, POOL], F32, "key_words")
        nc.sync.dma_start(result[:], base)
        grouped_q = interleave("grouped_q", raw_q[:])
        grouped_q2 = interleave("grouped_q2", raw_q2[:])
        mx_q = quantise("mx_q", grouped_q)
        mx_q2 = quantise("mx_q2", grouped_q2)
        a = product("a", mx_q, kw, ks)
        b = product("b", mx_q2, kw, ks)
        vw = gather("vw", val_words, U16)
        grouped_late = sbuf("grouped_late", [P, 2, ROWS, PACK], BF16)
        nc.scalar.copy(grouped_late[:], raw_late[:].rearrange("p o j q -> p o q j"))

        damped = sbuf("damped", [P, SLOTS], F32, "raw_late")
        damped_sum = sbuf("damped_sum", [P, 1], F32)
        nc.scalar.activation(damped[:], a[:], ACT.Exp, scale=damp[:], accum_out=damped_sum[:])
        neg_shift = sbuf("neg_shift", [P, 1], F32)
        nc.scalar.activation(
            neg_shift[:], damped_sum[:].bitcast(U32), ACT.Copy,
            scale=-UNDAMP * math.log(2.0) / 2.0**23, bias=UNDAMP * math.log(2.0) * 127.0,
        )
        pa = sbuf("pa", [P, SLOTS], F32)
        z = sbuf("z", [P, 1], F32)
        nc.scalar.activation(pa[:], a[:], ACT.Exp, bias=neg_shift[:], accum_out=z[:])

        b_max = sbuf("b_max", [P, PAGES], F32)
        nc.vector.tensor_reduce(b_max[:], paged(b[:]), AX.X, ALU.max)
        vs = gather("vs", val_scales, U8)
        late_codes = sbuf("late_codes", [P, 2 * ROWS], U32)
        late_scales = sbuf("late_scales", [P, 2 * ROWS], U8)
        nc.vector.quantize_mx(
            late_codes[:].bitcast(FP8X4), late_scales[:], grouped_late[:].rearrange("p o q j -> p (o q j)")
        )
        mx_dq = (late_codes[:, :ROWS], late_scales[:, :ROWS])
        mx_g = (late_codes[:, ROWS:], late_scales[:, ROWS:])
        b_shifted = sbuf("b_shifted", [P, SLOTS], F32)
        nc.vector.tensor_tensor(paged(b_shifted[:]), paged(b[:]), spread(b_max[:]), ALU.subtract)
        pb = sbuf("pb", [P, SLOTS], F32, "neg_shift")
        nc.scalar.activation(pb[:], b_shifted[:], ACT.Exp)
        ta = product("ta", mx_dq, kw, ks)
        c0 = product("c0", mx_g, vw, vs)

        z_inv = sbuf("z_inv", [P, 1], F32)
        nc.vector.reciprocal(z_inv[:], z[:])
        gain = sbuf("gain", [P, 1], F32)
        nc.scalar.activation(gain[:], z_inv[:], ACT.Copy, scale=GAIN)
        neg_z_inv = sbuf("neg_z_inv", [P, 1], F32)
        nc.scalar.activation(neg_z_inv[:], z_inv[:], ACT.Copy, scale=-1.0)
        p_sums = quad_sums("p_sums", [pa])
        tp = sbuf("tp", [P, SLOTS], F32)
        t_mean = sbuf("t_mean", [P, 1], F32)
        nc.vector.scalar_tensor_tensor(tp[:], ta[:], z_inv[:], pa[:], ALU.mult, ALU.mult, accum_out=t_mean[:])
        x = sbuf("x", [P, SLOTS], F32)
        nc.vector.scalar_tensor_tensor(x[:], ta[:], t_mean[:], pa[:], ALU.subtract, ALU.mult)
        sb = sbuf("sb", [P, PAGES], F32)
        nc.vector.tensor_reduce(sb[:], paged(pb[:]), AX.X, ALU.add)
        drr = sbuf("drr", [P, SLOTS], F32)
        nc.vector.scalar_tensor_tensor(drr[:], c0[:], gain[:], pb[:], ALU.mult, ALU.mult)
        sb_inv = sbuf("sb_inv", [P, PAGES], F32)
        sb_rsqrt = sbuf("sb_rsqrt", [P, PAGES], F32)
        nc.scalar.activation(sb_rsqrt[:], sb[:], ACT.Abs_reciprocal_sqrt)
        nc.scalar.activation(sb_inv[:], sb_rsqrt[:], ACT.Square)
        dr = sbuf("dr", [P, PAGES], F32)
        nc.vector.tensor_reduce(dr[:], paged(drr[:]), AX.X, ALU.add)
        xs = sbuf("xs", [P, PAGES], F32)
        nc.vector.tensor_reduce(xs[:], paged(x[:]), AX.X, ALU.add)
        u = sbuf("u", [P, PAGES], F32)
        nc.vector.tensor_tensor(u[:], dr[:], sb_inv[:], ALU.mult)
        c_terms = sbuf("c_terms", [P, PAGES], F32)
        offset_c = sbuf("offset_c", [P, 1], F32)
        nc.vector.scalar_tensor_tensor(
            c_terms[:], xs[:], neg_z_inv[:], u[:], ALU.mult, ALU.mult, accum_out=offset_c[:]
        )
        u_terms = sbuf("u_terms", [P, P], F32)
        u_mean = sbuf("u_mean", [P, 1], F32)
        nc.vector.scalar_tensor_tensor(
            halves(u_terms[:]), halves(p_sums[:, 0, :]), z_inv[:], spread2(u[:]), ALU.mult, ALU.mult,
            accum_out=u_mean[:],
        )
        along_pa = sbuf("along_pa", [P, SLOTS], F32)
        nc.scalar.activation(along_pa[:], pa[:], ACT.Copy, scale=offset_c[:])
        along_x = sbuf("along_x", [P, SLOTS], F32)
        nc.vector.scalar_tensor_tensor(
            paged(along_x[:]), spread(u[:]), u_mean[:], paged(x[:]), ALU.subtract, ALU.mult
        )
        nc.vector.tensor_tensor(placed[:].indirect(offsets[:]), along_x[:], along_pa[:], ALU.add)

        start = 0
        for n, width in enumerate(STORE_WIDTHS):
            cols = slice(start, start + width)
            nc.vector.tensor_tensor(result[:, cols], result[:, cols], placed[:, cols], ALU.add)
            queue = nc.sync if n % 2 == 0 else nc.scalar
            queue.dma_start(out[:, cols], result[:, cols])
            start += width
